import numpy as np
import ml_dtypes


def mxq(x, axis, fmt="e4m3"):
    dtype, down = {"e4m3": (ml_dtypes.float8_e4m3fn, 7), "e5m2": (ml_dtypes.float8_e5m2, 14)}[fmt]
    v = np.moveaxis(np.asarray(x, np.float32).astype(ml_dtypes.bfloat16).astype(np.float64), axis, -1)
    blocks = v.reshape(v.shape[:-1] + (-1, 32))
    amax = np.abs(blocks).max(-1, keepdims=True)
    byte = np.maximum(np.where(amax > 0, np.frexp(amax)[1] - 1 + 127, 0) - down, 1)
    scale = np.exp2(byte - 127.0)
    codes = (blocks / scale).astype(np.float32).astype(dtype).astype(np.float64)
    return np.moveaxis((codes * scale).reshape(v.shape), -1, axis)


WIDE = False


def mx_kscale(k):
    if not WIDE:
        return np.ones(k)
    levels = np.array([10, -10, 5, -5, 0])
    if k % 512:
        return np.exp2(np.random.permutation(np.resize(levels, k // 32))).repeat(32)
    a = np.empty((k // 512, 16))
    for p in range(k // 512):
        a[p, :8] = np.random.permutation(np.resize(levels, 8))
        for g in range(8):
            far = levels[np.abs(levels - a[p, g]) >= 10]
            a[p, g + 8] = far[np.random.randint(len(far))]
    return np.exp2(a.ravel()).repeat(32)


def f64(x):
    return np.asarray(x).astype(np.float64)


def striped(idx):
    return np.tile(np.asarray(idx).reshape(-1, 16).T, (8, 1)).astype(np.uint16)


def unstriped(offs):
    return offs[:16].T.reshape(-1).astype(np.int64)


E2M1 = np.array([0.0, 0.5, 1.0, 1.5, 2.0, 3.0, 4.0, 6.0, -0.0, -0.5, -1.0, -1.5, -2.0, -3.0, -4.0, -6.0])


def pack_weight(w, fmt):
    k, n = w.shape
    w = f64(np.asarray(w, np.float32).astype(ml_dtypes.bfloat16)).reshape(k // 32, 32, n)
    amax = np.abs(w).max(1)
    if fmt == "e4m3":
        byte = np.frexp(amax)[1] - 1 + 127 - 7
    else:
        mant, ex = np.frexp(amax / 6.0)
        byte = np.where(mant > 0.5, ex, ex - 1) + 127
    byte = np.clip(np.where(amax > 0, byte, 1), 1, 254)
    scaled = (w * np.exp2(127.0 - byte)[:, None, :]).reshape(k, n).astype(np.float32)
    by_word = np.ascontiguousarray(scaled.reshape(k // 512, 128, 4, n).transpose(0, 1, 3, 2))
    if fmt == "e4m3":
        words = by_word.astype(ml_dtypes.float8_e4m3fn).view(np.uint8)
    else:
        c = by_word.astype(ml_dtypes.float4_e2m1fn).view(np.uint8) & 0xF
        words = (c[..., 0::2] | (c[..., 1::2] << 4)).reshape(k // 512, 128, 2 * n)
    return np.ascontiguousarray(words), np.ascontiguousarray(byte.astype(np.uint8).reshape(k // 512, 16, n))


def unpack_weight(words, scales, fmt):
    g, _, n = scales.shape
    words = np.ascontiguousarray(words).reshape(g, 128, n, -1)
    if fmt == "e4m3":
        vals = words.view(ml_dtypes.float8_e4m3fn).astype(np.float64)
    else:
        nib = np.empty((g, 128, n, 4), np.uint8)
        nib[..., 0::2] = words & 0xF
        nib[..., 1::2] = words >> 4
        vals = E2M1[nib]
    vals = vals * np.repeat(np.exp2(scales.astype(np.float64) - 127.0), 8, axis=1)[..., None]
    return vals.transpose(0, 1, 3, 2).reshape(g * 512, n)


def bf(x):
    return np.asarray(x, np.float32).astype(ml_dtypes.bfloat16)


def planes(Y):
    r, m = Y.shape
    b = f64(bf(Y)).reshape(r // 32, 32, m)
    amax = np.abs(b).max(1)
    byte = np.clip(np.where(amax > 0, np.frexp(amax)[1] - 1 + 127 - 7, 1), 1, 254)
    codes = (b * np.exp2(127.0 - byte)[:, None, :]).reshape(r, m).astype(np.float32).astype(ml_dtypes.float8_e4m3fn).view(np.uint8)
    words = codes.reshape(r // 512, 128, 4, m).transpose(0, 1, 3, 2)
    return np.ascontiguousarray(words), np.ascontiguousarray(byte.astype(np.uint8).reshape(r // 512, 16, m))


B, N, T, D, NQ = 1, 512, 2048, 1024, 512


def setup_inputs():
    n = np.random.standard_normal
    idx = np.random.permutation(T)[:B * N]
    s = mx_kscale(D)[:, None]
    kp = pack_weight(n((D, T)) / s, "e2m1")
    return {
        "qT": (n((B, D, NQ)) * s * (1.00 / np.sqrt(D))).astype(np.float32),
        "k_words": np.ascontiguousarray(kp[0].reshape(1, 2, 128, T, 2).transpose(0, 2, 3, 1, 4)).reshape(1, 128, T, 4),
        "k_scales": kp[1],
        "ls": (np.random.uniform(7.8, 8.4, (B, 1, NQ))).astype(np.float32),
        "mk": (np.random.uniform(size=(B, N, NQ)) < 0.5).astype(np.float32),
        "offs": striped(idx),
    }


def reference(qT, k_words, k_scales, ls, mk, offs):
    idx = unstriped(offs)
    pick = lambda x, which: x[:, which].reshape(x.shape[0], B, -1).transpose(1, 0, 2)
    k = unpack_weight(k_words.reshape(1, 128, T, 2, 2).transpose(0, 3, 1, 2, 4).reshape(2, 128, 2 * T), k_scales, "e2m1")
    kg = pick(k, idx)
    qq = mxq(f64(qT), 1, "e4m3")
    a = kg.transpose(0, 2, 1) @ qq
    y = np.exp(a - f64(ls)) * f64(mk)
    Y = y[0]
    words, scales = planes(Y)
    return Y, words, scales

@@ -1,0 +1,166 @@
+from contextlib import ExitStack
+
+import concourse.mybir as mybir
+
+SLOTS, TOKENS, FEATURES, QUERIES = 512, 2048, 1024, 512
+FLOPS = 2 * SLOTS * FEATURES * QUERIES
+
+F32 = mybir.dt.float32
+BF16 = mybir.dt.bfloat16
+I32 = mybir.dt.int32
+U32 = mybir.dt.uint32
+U16 = mybir.dt.uint16
+U8 = mybir.dt.uint8
+FP8X4 = mybir.dt.float8_e4m3fn_x4
+FP4X4 = mybir.dt.float4_e2m1fn_x4
+EXP = mybir.ActivationFunctionType.Exp
+MULT = mybir.AluOpType.mult
+
+P = 128
+PACK = 4
+PASSES = FEATURES // (P * PACK)
+HALF = QUERIES // 2
+BLOCKS = QUERIES // P
+
+
+def interleave(engine_copy, dst, src):
+    engine_copy(
+        dst.rearrange("p (c i) t -> p c t i", i=PACK),
+        src.rearrange("p t (c i) -> p c t i", i=PACK),
+    )
+
+
+def tile_attend_plw_mask_topk_kernel(tc, qT, k_words, k_scales, ls, mk, offs, out_0, out_1, out_2):
+    nc = tc.nc
+    with ExitStack() as ctx:
+        sb = ctx.enter_context(tc.tile_pool(name="sb", bufs=1))
+        stage = ctx.enter_context(tc.tile_pool(name="stage", bufs=1))
+        ps = ctx.enter_context(tc.psum_pool(name="ps", bufs=4))
+
+        offsets = sb.tile([P, SLOTS // 16], U16, name="offsets")
+        nc.sync.dma_start(offsets[:], offs)
+
+        piece = PACK * HALF
+        ls_rows = sb.tile([P, P], F32, name="ls_rows")
+        nc.gpsimd.memset(ls_rows[:], 0.0)
+        nc.sync.dma_start(ls_rows[0:BLOCKS, :], ls[0, 0].rearrange("(j p) -> j p", p=P))
+
+        pool_scales = sb.tile([P, PASSES * TOKENS // 4], I32, name="pool_scales", align_bytes=64)
+        nc.vector.memset(pool_scales[:], 0)
+        for quad in (0, 2, 1, 3):
+            nc.sync.dma_start(
+                pool_scales[32 * quad:32 * quad + 4, :].rearrange("f (o t) -> f o t", o=PASSES),
+                k_scales.bitcast(I32)[:, 4 * quad:4 * quad + 4, :].rearrange("o f t -> f o t"),
+            )
+
+        q_rows = qT[0].rearrange("(o p t) q -> o p t q", p=P, t=PACK)
+        mk_rows = mk[0].rearrange("(p r) q -> p r q", r=PACK)
+        q_raw, q_codes, q_scales, mask = {}, {}, {}, {}
+
+        def load_q(h, o, place):
+            q_raw[h, o] = place.rearrange("p (t q) -> p t q", t=PACK)
+            nc.sync.dma_start(q_raw[h, o], q_rows[o, :, :, h * HALF:(h + 1) * HALF])
+
+        def load_mask(h, place):
+            mask[h] = place.rearrange("p (r q) -> p r q", r=PACK)
+            nc.sync.dma_start(mask[h], mk_rows[:, :, h * HALF:(h + 1) * HALF])
+
+        def quantise_q(h, o, engine_copy):
+            grouped = sb.tile([P, HALF, PACK], BF16, name="q_grouped_%d_%d" % (h, o), align_bytes=64)
+            interleave(engine_copy, grouped[:], q_raw[h, o])
+            q_codes[h, o] = sb.tile([P, HALF], U32, name="q_codes_%d_%d" % (h, o), align_bytes=64)
+            q_scales[h, o] = sb.tile([P, HALF], U8, name="q_scales_%d_%d" % (h, o), align_bytes=64)
+            nc.vector.quantize_mx(
+                out=q_codes[h, o][:].bitcast(FP8X4),
+                scales=q_scales[h, o][:],
+                in_=grouped[:].rearrange("p c t -> p (c t)"),
+            )
+
+        first = sb.tile([P, piece], F32, name="first")
+        load_q(0, 0, first[:])
+
+        identity = sb.tile([P, P], F32, name="identity")
+        blank = stage.tile([P, 7 * piece], F32, name="blank", offset=0)
+        nc.gpsimd.memset(blank[:, 0:P], 0.0)
+        nc.gpsimd.affine_select(
+            out=identity[:], in_=blank[:, 0:P], compare_op=mybir.AluOpType.not_equal, fill=1.0,
+            base=0, pattern=[[-1, P]], channel_multiplier=1,
+        )
+        ls_turned = ps.tile([P, PACK, P], F32, name="ls_turned", tag="turned")
+        nc.tensor.transpose(ls_turned[:, 0, :], ls_rows[:], identity[:])
+        minus_ls = sb.tile([P, BLOCKS], F32, name="minus_ls")
+        nc.vector.tensor_scalar_mul(minus_ls[:], ls_turned[:, 0, 0:BLOCKS], -1.0)
+        warm = sb.tile([P, 1], F32, name="warm")
+        nc.scalar.activation(warm[:], minus_ls[:, 0:1], EXP)
+
+        pool_words = stage.tile([P, TOKENS], I32, name="pool_words", offset=4 * piece * 5)
+        nc.sync.dma_start(pool_words[:], k_words[0].rearrange("p t b -> p (t b)").bitcast(I32))
+        later = [stage.tile([P, piece], F32, name="later_%d" % n, offset=4 * piece * n) for n in range(5)]
+        load_q(0, 1, later[0][:])
+        load_q(1, 0, later[1][:])
+        load_q(1, 1, later[2][:])
+        load_mask(0, later[3][:])
+        load_mask(1, later[4][:])
+        quantise_q(0, 0, nc.scalar.copy)
+
+        key_scales = []
+        for o in range(PASSES):
+            key_scales.append(sb.tile([P, SLOTS], U8, name="key_scales_%d" % o, align_bytes=64))
+            nc.vector.tensor_copy(
+                key_scales[o][:], pool_scales[:].bitcast(U8)[:, o * TOKENS:(o + 1) * TOKENS].indirect(offsets[:])
+            )
+        key_pairs = sb.tile([P, SLOTS], U32, name="key_pairs", align_bytes=64)
+        nc.vector.tensor_copy(key_pairs[:], pool_words[:].bitcast(U32).indirect(offsets[:]))
+        key_codes = sb.tile([P, PASSES * 2 * SLOTS], U8, name="key_codes", align_bytes=64)
+        nc.vector.tensor_copy(
+            key_codes[:].bitcast(U16).rearrange("p (o n) -> p o n", o=PASSES),
+            key_pairs[:].bitcast(U16).rearrange("p (n o) -> p o n", o=PASSES),
+        )
+
+        quantise_q(0, 1, nc.scalar.copy)
+        quantise_q(1, 0, nc.scalar.copy)
+        quantise_q(1, 1, nc.vector.tensor_copy)
+
+        y_rows = out_0.rearrange("(p r) q -> p r q", r=PACK)
+        y_words = out_1[0].rearrange("p q b -> p (q b)").bitcast(I32)
+        y_codes = sb.tile([P, QUERIES], I32, name="y_codes", align_bytes=64)
+        y_scales = sb.tile([P, QUERIES], U8, name="y_scales", align_bytes=64)
+
+        for h in range(2):
+            y = sb.tile([P, PACK, HALF], F32, name="y_%d" % h)
+            for j in (2 * h, 2 * h + 1):
+                cols = slice((j % 2) * P, (j % 2 + 1) * P)
+                scores = ps.tile([P, SLOTS], F32, name="scores")
+                for o in range(PASSES):
+                    nc.tensor.matmul_mx(
+                        out=scores[:],
+                        lhsT=q_codes[h, o][:, cols].bitcast(FP8X4),
+                        lhsT_scale=q_scales[h, o][:, cols],
+                        rhs=key_codes[:, o * 2 * SLOTS:(o + 1) * 2 * SLOTS].bitcast(FP4X4),
+                        rhs_scale=key_scales[o][:],
+                        start=(o == 0),
+                        stop=(o == PASSES - 1),
+                    )
+                weights = sb.tile([P, PACK, P], F32, name="weights_%d" % j)
+                nc.scalar.activation(
+                    weights[:], scores[:].rearrange("q (s r) -> q r s", r=PACK), EXP, bias=minus_ls[:, j:j + 1]
+                )
+                turned = ps.tile([P, PACK, P], F32, name="turned", tag="turned")
+                for r in range(PACK):
+                    nc.tensor.transpose(turned[:, r, :], weights[:, r, :], identity[:])
+                nc.vector.tensor_tensor(y[:, :, cols], turned[:], mask[h][:, :, cols], MULT)
+            nc.sync.dma_start(y_rows[:, :, h * HALF:(h + 1) * HALF], y[:])
+            for j in (2 * h, 2 * h + 1):
+                cols = slice((j % 2) * P, (j % 2 + 1) * P)
+                y_grouped = sb.tile([P, P, PACK], BF16, name="y_grouped_%d" % j, align_bytes=64)
+                interleave(nc.scalar.copy if j in (1, 2) else nc.vector.tensor_copy, y_grouped[:], y[:, :, cols])
+                nc.vector.quantize_mx(
+                    out=y_codes[:, j * P:(j + 1) * P].bitcast(FP8X4),
+                    scales=y_scales[:, j * P:(j + 1) * P],
+                    in_=y_grouped[:].rearrange("p c t -> p (c t)"),
+                )
+            nc.sync.dma_start(y_words[:, h * HALF:(h + 1) * HALF], y_codes[:, h * HALF:(h + 1) * HALF])
+        for quad in range(4):
+            nc.scalar.dma_start(
+                out_2[0].bitcast(I32)[4 * quad:4 * quad + 4, :], y_scales[32 * quad:32 * quad + 4, :].bitcast(I32)
+            )

@@ -35,6 +35,7 @@ def tile_attend_plw_mask_topk_kernel(tc, qT, k_words, k_scales, ls, mk, offs, ou
     with ExitStack() as ctx:
         sb = ctx.enter_context(tc.tile_pool(name="sb", bufs=1))
         stage = ctx.enter_context(tc.tile_pool(name="stage", bufs=1))
+        reuse = ctx.enter_context(tc.tile_pool(name="reuse", bufs=1))
         ps = ctx.enter_context(tc.psum_pool(name="ps", bufs=4))
 
         offsets = sb.tile([P, SLOTS // 16], U16, name="offsets")
@@ -45,7 +46,7 @@ def tile_attend_plw_mask_topk_kernel(tc, qT, k_words, k_scales, ls, mk, offs, ou
         nc.gpsimd.memset(ls_rows[:], 0.0)
         nc.sync.dma_start(ls_rows[0:BLOCKS, :], ls[0, 0].rearrange("(j p) -> j p", p=P))
 
-        pool_scales = sb.tile([P, PASSES * TOKENS // 4], I32, name="pool_scales", align_bytes=64)
+        pool_scales = reuse.tile([P, PASSES * TOKENS // 4], I32, name="pool_scales", align_bytes=64, offset=0)
         nc.vector.memset(pool_scales[:], 0)
         for quad in (0, 2, 1, 3):
             nc.sync.dma_start(
@@ -65,16 +66,18 @@ def tile_attend_plw_mask_topk_kernel(tc, qT, k_words, k_scales, ls, mk, offs, ou
             mask[h] = place.rearrange("p (r q) -> p r q", r=PACK)
             nc.sync.dma_start(mask[h], mk_rows[:, :, h * HALF:(h + 1) * HALF])
 
-        def quantise_q(h, o, engine_copy):
-            grouped = sb.tile([P, HALF, PACK], BF16, name="q_grouped_%d_%d" % (h, o), align_bytes=64)
-            interleave(engine_copy, grouped[:], q_raw[h, o])
-            q_codes[h, o] = sb.tile([P, HALF], U32, name="q_codes_%d_%d" % (h, o), align_bytes=64)
+        def quantise_q(h, o, engine_copy, codes, widths):
+            grouped = sb.tile([P, HALF, PACK], BF16, name="q_grouped", bufs=2, align_bytes=64)
+            q_codes[h, o] = codes
             q_scales[h, o] = sb.tile([P, HALF], U8, name="q_scales_%d_%d" % (h, o), align_bytes=64)
-            nc.vector.quantize_mx(
-                out=q_codes[h, o][:].bitcast(FP8X4),
-                scales=q_scales[h, o][:],
-                in_=grouped[:].rearrange("p c t -> p (c t)"),
-            )
+            for c in range(0, HALF, widths):
+                interleave(engine_copy, grouped[:, c:c + widths, :], q_raw[h, o][:, :, c:c + widths])
+            for c in range(0, HALF, widths):
+                nc.vector.quantize_mx(
+                    out=q_codes[h, o][:, c:c + widths].bitcast(FP8X4),
+                    scales=q_scales[h, o][:, c:c + widths],
+                    in_=grouped[:, c:c + widths, :].rearrange("p c t -> p (c t)"),
+                )
 
         first = sb.tile([P, piece], F32, name="first")
         load_q(0, 0, first[:])
@@ -101,7 +104,6 @@ def tile_attend_plw_mask_topk_kernel(tc, qT, k_words, k_scales, ls, mk, offs, ou
         load_q(1, 1, later[2][:])
         load_mask(0, later[3][:])
         load_mask(1, later[4][:])
-        quantise_q(0, 0, nc.scalar.copy)
 
         key_scales = []
         for o in range(PASSES):
@@ -109,28 +111,31 @@ def tile_attend_plw_mask_topk_kernel(tc, qT, k_words, k_scales, ls, mk, offs, ou
             nc.vector.tensor_copy(
                 key_scales[o][:], pool_scales[:].bitcast(U8)[:, o * TOKENS:(o + 1) * TOKENS].indirect(offsets[:])
             )
-        key_pairs = sb.tile([P, SLOTS], U32, name="key_pairs", align_bytes=64)
+        quantise_q(0, 0, nc.scalar.copy, reuse.tile([P, HALF], U32, name="q_codes_00", align_bytes=64, offset=8 * HALF), HALF)
+        key_pairs = reuse.tile([P, SLOTS], U32, name="key_pairs", align_bytes=64, offset=0)
         nc.vector.tensor_copy(key_pairs[:], pool_words[:].bitcast(U32).indirect(offsets[:]))
         key_codes = sb.tile([P, PASSES * 2 * SLOTS], U8, name="key_codes", align_bytes=64)
-        nc.vector.tensor_copy(
-            key_codes[:].bitcast(U16).rearrange("p (o n) -> p o n", o=PASSES),
-            key_pairs[:].bitcast(U16).rearrange("p (n o) -> p o n", o=PASSES),
-        )
+        for o in range(PASSES):
+            nc.vector.tensor_copy(
+                key_codes[:].bitcast(U16)[:, o * SLOTS:(o + 1) * SLOTS],
+                key_pairs[:].bitcast(U16).rearrange("p (n o) -> p o n", o=PASSES)[:, o, :],
+            )
 
-        quantise_q(0, 1, nc.scalar.copy)
-        quantise_q(1, 0, nc.scalar.copy)
-        quantise_q(1, 1, nc.vector.tensor_copy)
+        quantise_q(0, 1, nc.scalar.copy, reuse.tile([P, HALF], U32, name="q_codes_01", align_bytes=64, offset=0), HALF)
+        quantise_q(1, 0, nc.scalar.copy, reuse.tile([P, HALF], U32, name="q_codes_10", align_bytes=64, offset=4 * HALF), HALF)
+        quantise_q(1, 1, nc.vector.tensor_copy, sb.tile([P, HALF], U32, name="q_codes_11", align_bytes=64), P)
 
         y_rows = out_0.rearrange("(p r) q -> p r q", r=PACK)
         y_words = out_1[0].rearrange("p q b -> p (q b)").bitcast(I32)
         y_codes = sb.tile([P, QUERIES], I32, name="y_codes", align_bytes=64)
         y_scales = sb.tile([P, QUERIES], U8, name="y_scales", align_bytes=64)
 
+        grouped_halves = []
         for h in range(2):
             y = sb.tile([P, PACK, HALF], F32, name="y_%d" % h)
             for j in (2 * h, 2 * h + 1):
                 cols = slice((j % 2) * P, (j % 2 + 1) * P)
-                scores = ps.tile([P, SLOTS], F32, name="scores")
+                scores = ps.tile([P, SLOTS], F32, name="scores", bufs=3)
                 for o in range(PASSES):
                     nc.tensor.matmul_mx(
                         out=scores[:],
@@ -150,17 +155,20 @@ def tile_attend_plw_mask_topk_kernel(tc, qT, k_words, k_scales, ls, mk, offs, ou
                     nc.tensor.transpose(turned[:, r, :], weights[:, r, :], identity[:])
                 nc.vector.tensor_tensor(y[:, :, cols], turned[:], mask[h][:, :, cols], MULT)
             nc.sync.dma_start(y_rows[:, :, h * HALF:(h + 1) * HALF], y[:])
-            for j in (2 * h, 2 * h + 1):
-                cols = slice((j % 2) * P, (j % 2 + 1) * P)
-                y_grouped = sb.tile([P, P, PACK], BF16, name="y_grouped_%d" % j, align_bytes=64)
-                interleave(nc.scalar.copy if j in (1, 2) else nc.vector.tensor_copy, y_grouped[:], y[:, :, cols])
-                nc.vector.quantize_mx(
-                    out=y_codes[:, j * P:(j + 1) * P].bitcast(FP8X4),
-                    scales=y_scales[:, j * P:(j + 1) * P],
-                    in_=y_grouped[:].rearrange("p c t -> p (c t)"),
-                )
+            y_grouped = sb.tile([P, HALF, PACK], BF16, name="y_grouped_%d" % h, align_bytes=64)
+            for c in range(0, HALF, P):
+                on_vector = (h * HALF + c) in (0, QUERIES - P)
+                interleave(nc.vector.tensor_copy if on_vector else nc.scalar.copy, y_grouped[:, c:c + P, :], y[:, :, c:c + P])
+            grouped_halves.append(y_grouped)
+        for h in range(2):
+            nc.vector.quantize_mx(
+                out=y_codes[:, h * HALF:(h + 1) * HALF].bitcast(FP8X4),
+                scales=y_scales[:, h * HALF:(h + 1) * HALF],
+                in_=grouped_halves[h][:].rearrange("p c t -> p (c t)"),
+            )
             nc.sync.dma_start(y_words[:, h * HALF:(h + 1) * HALF], y_codes[:, h * HALF:(h + 1) * HALF])
         for quad in range(4):
-            nc.scalar.dma_start(
+            queue = nc.scalar if quad < 2 else nc.sync
+            queue.dma_start(
                 out_2[0].bitcast(I32)[4 * quad:4 * quad + 4, :], y_scales[32 * quad:32 * quad + 4, :].bitcast(I32)
             )

@@ -14,6 +14,7 @@ U8 = mybir.dt.uint8
 FP8X4 = mybir.dt.float8_e4m3fn_x4
 FP4X4 = mybir.dt.float4_e2m1fn_x4
 EXP = mybir.ActivationFunctionType.Exp
+COPY = mybir.ActivationFunctionType.Copy
 MULT = mybir.AluOpType.mult
 
 P = 128
@@ -36,7 +37,8 @@ def tile_attend_plw_mask_topk_kernel(tc, qT, k_words, k_scales, ls, mk, offs, ou
         sb = ctx.enter_context(tc.tile_pool(name="sb", bufs=1))
         stage = ctx.enter_context(tc.tile_pool(name="stage", bufs=1))
         reuse = ctx.enter_context(tc.tile_pool(name="reuse", bufs=1))
-        ps = ctx.enter_context(tc.psum_pool(name="ps", bufs=4))
+        late = ctx.enter_context(tc.tile_pool(name="late", bufs=1))
+        ps = ctx.enter_context(tc.psum_pool(name="ps", bufs=BLOCKS))
 
         offsets = sb.tile([P, SLOTS // 16], U16, name="offsets")
         nc.sync.dma_start(offsets[:], offs)
@@ -66,17 +68,18 @@ def tile_attend_plw_mask_topk_kernel(tc, qT, k_words, k_scales, ls, mk, offs, ou
             mask[h] = place.rearrange("p (r q) -> p r q", r=PACK)
             nc.sync.dma_start(mask[h], mk_rows[:, :, h * HALF:(h + 1) * HALF])
 
-        def quantise_q(h, o, engine_copy, codes, widths):
+        def quantise_q(h, o, engine_copies, codes):
+            width = HALF // len(engine_copies)
             grouped = sb.tile([P, HALF, PACK], BF16, name="q_grouped", bufs=2, align_bytes=64)
             q_codes[h, o] = codes
             q_scales[h, o] = sb.tile([P, HALF], U8, name="q_scales_%d_%d" % (h, o), align_bytes=64)
-            for c in range(0, HALF, widths):
-                interleave(engine_copy, grouped[:, c:c + widths, :], q_raw[h, o][:, :, c:c + widths])
-            for c in range(0, HALF, widths):
+            for c, engine_copy in zip(range(0, HALF, width), engine_copies):
+                interleave(engine_copy, grouped[:, c:c + width, :], q_raw[h, o][:, :, c:c + width])
+            for c in range(0, HALF, width):
                 nc.vector.quantize_mx(
-                    out=q_codes[h, o][:, c:c + widths].bitcast(FP8X4),
-                    scales=q_scales[h, o][:, c:c + widths],
-                    in_=grouped[:, c:c + widths, :].rearrange("p c t -> p (c t)"),
+                    out=q_codes[h, o][:, c:c + width].bitcast(FP8X4),
+                    scales=q_scales[h, o][:, c:c + width],
+                    in_=grouped[:, c:c + width, :].rearrange("p c t -> p (c t)"),
                 )
 
         first = sb.tile([P, piece], F32, name="first")
@@ -91,10 +94,8 @@ def tile_attend_plw_mask_topk_kernel(tc, qT, k_words, k_scales, ls, mk, offs, ou
         )
         ls_turned = ps.tile([P, PACK, P], F32, name="ls_turned", tag="turned")
         nc.tensor.transpose(ls_turned[:, 0, :], ls_rows[:], identity[:])
-        minus_ls = sb.tile([P, BLOCKS], F32, name="minus_ls")
-        nc.vector.tensor_scalar_mul(minus_ls[:], ls_turned[:, 0, 0:BLOCKS], -1.0)
-        warm = sb.tile([P, 1], F32, name="warm")
-        nc.scalar.activation(warm[:], minus_ls[:, 0:1], EXP)
+        minus_ls = late.tile([P, BLOCKS], F32, name="minus_ls", align_bytes=64, offset=0)
+        nc.scalar.activation(minus_ls[:], ls_turned[:, 0, 0:BLOCKS], COPY, scale=-1.0)
 
         pool_words = stage.tile([P, TOKENS], I32, name="pool_words", offset=4 * piece * 5)
         nc.sync.dma_start(pool_words[:], k_words[0].rearrange("p t b -> p (t b)").bitcast(I32))
@@ -111,62 +112,97 @@ def tile_attend_plw_mask_topk_kernel(tc, qT, k_words, k_scales, ls, mk, offs, ou
             nc.vector.tensor_copy(
                 key_scales[o][:], pool_scales[:].bitcast(U8)[:, o * TOKENS:(o + 1) * TOKENS].indirect(offsets[:])
             )
-        quantise_q(0, 0, nc.scalar.copy, reuse.tile([P, HALF], U32, name="q_codes_00", align_bytes=64, offset=8 * HALF), HALF)
         key_pairs = reuse.tile([P, SLOTS], U32, name="key_pairs", align_bytes=64, offset=0)
         nc.vector.tensor_copy(key_pairs[:], pool_words[:].bitcast(U32).indirect(offsets[:]))
-        key_codes = sb.tile([P, PASSES * 2 * SLOTS], U8, name="key_codes", align_bytes=64)
+        quantise_q(0, 0, [nc.scalar.copy], reuse.tile([P, HALF], U32, name="q_codes_00", align_bytes=64, offset=8 * HALF))
+        key_codes = []
         for o in range(PASSES):
+            key_codes.append(sb.tile([P, 2 * SLOTS], U8, name="key_codes_%d" % o, align_bytes=64))
             nc.vector.tensor_copy(
-                key_codes[:].bitcast(U16)[:, o * SLOTS:(o + 1) * SLOTS],
+                key_codes[o][:].bitcast(U16),
                 key_pairs[:].bitcast(U16).rearrange("p (n o) -> p o n", o=PASSES)[:, o, :],
             )
 
-        quantise_q(0, 1, nc.scalar.copy, reuse.tile([P, HALF], U32, name="q_codes_01", align_bytes=64, offset=0), HALF)
-        quantise_q(1, 0, nc.scalar.copy, reuse.tile([P, HALF], U32, name="q_codes_10", align_bytes=64, offset=4 * HALF), HALF)
-        quantise_q(1, 1, nc.vector.tensor_copy, sb.tile([P, HALF], U32, name="q_codes_11", align_bytes=64), P)
+        quantise_q(0, 1, [nc.scalar.copy], reuse.tile([P, HALF], U32, name="q_codes_01", align_bytes=64, offset=0))
+        quantise_q(1, 0, [nc.scalar.copy], reuse.tile([P, HALF], U32, name="q_codes_10", align_bytes=64, offset=4 * HALF))
+        quantise_q(1, 1, [nc.vector.tensor_copy, nc.scalar.copy], sb.tile([P, HALF], U32, name="q_codes_11", align_bytes=64))
 
+        def half_and_columns(j):
+            return j // 2, slice((j % 2) * P, (j % 2 + 1) * P)
+
+        scores = [ps.tile([P, SLOTS], F32, name="scores") for j in range(BLOCKS)]
+        weights = [sb.tile([P, PACK, P], F32, name="weights_%d" % j) for j in range(BLOCKS)]
+        y = [sb.tile([P, PACK, HALF], F32, name="y_%d" % h) for h in range(2)]
         y_rows = out_0.rearrange("(p r) q -> p r q", r=PACK)
+
+        def score_pass(h, o):
+            for j in (2 * h, 2 * h + 1):
+                cols = half_and_columns(j)[1]
+                nc.tensor.matmul_mx(
+                    out=scores[j][:],
+                    lhsT=q_codes[h, o][:, cols].bitcast(FP8X4),
+                    lhsT_scale=q_scales[h, o][:, cols],
+                    rhs=key_codes[o][:].bitcast(FP4X4),
+                    rhs_scale=key_scales[o][:],
+                    start=(o == 0),
+                    stop=(o == PASSES - 1),
+                )
+
+        def exponentiate(j):
+            nc.scalar.activation(
+                weights[j][:], scores[j][:].rearrange("q (s r) -> q r s", r=PACK), EXP, bias=minus_ls[:, j:j + 1]
+            )
+
+        def turn_and_mask(j):
+            h, cols = half_and_columns(j)
+            turned = ps.tile([P, PACK, P], F32, name="turned", tag="turned")
+            for r in range(PACK):
+                nc.tensor.transpose(turned[:, r, :], weights[j][:, r, :], identity[:])
+            nc.vector.tensor_tensor(y[h][:, :, cols], turned[:], mask[h][:, :, cols], MULT)
+            if j % 2 == 1:
+                nc.sync.dma_start(y_rows[:, :, h * HALF:(h + 1) * HALF], y[h][:])
+
+        score_pass(0, 0)
+        score_pass(0, 1)
+        score_pass(1, 0)
+        exponentiate(0)
+        exponentiate(1)
+        turn_and_mask(0)
+        score_pass(1, 1)
+        exponentiate(2)
+        exponentiate(3)
+        for j in range(1, BLOCKS):
+            turn_and_mask(j)
+
         y_words = out_1[0].rearrange("p q b -> p (q b)").bitcast(I32)
         y_codes = sb.tile([P, QUERIES], I32, name="y_codes", align_bytes=64)
         y_scales = sb.tile([P, QUERIES], U8, name="y_scales", align_bytes=64)
+        y_grouped = [
+            late.tile([P, P, PACK], BF16, name="y_grouped_%d" % j, align_bytes=64, offset=2 * P * PACK * ((j - 1) % BLOCKS))
+            for j in range(BLOCKS)
+        ]
 
-        grouped_halves = []
-        for h in range(2):
-            y = sb.tile([P, PACK, HALF], F32, name="y_%d" % h)
-            for j in (2 * h, 2 * h + 1):
-                cols = slice((j % 2) * P, (j % 2 + 1) * P)
-                scores = ps.tile([P, SLOTS], F32, name="scores", bufs=3)
-                for o in range(PASSES):
-                    nc.tensor.matmul_mx(
-                        out=scores[:],
-                        lhsT=q_codes[h, o][:, cols].bitcast(FP8X4),
-                        lhsT_scale=q_scales[h, o][:, cols],
-                        rhs=key_codes[:, o * 2 * SLOTS:(o + 1) * 2 * SLOTS].bitcast(FP4X4),
-                        rhs_scale=key_scales[o][:],
-                        start=(o == 0),
-                        stop=(o == PASSES - 1),
-                    )
-                weights = sb.tile([P, PACK, P], F32, name="weights_%d" % j)
-                nc.scalar.activation(
-                    weights[:], scores[:].rearrange("q (s r) -> q r s", r=PACK), EXP, bias=minus_ls[:, j:j + 1]
-                )
-                turned = ps.tile([P, PACK, P], F32, name="turned", tag="turned")
-                for r in range(PACK):
-                    nc.tensor.transpose(turned[:, r, :], weights[:, r, :], identity[:])
-                nc.vector.tensor_tensor(y[:, :, cols], turned[:], mask[h][:, :, cols], MULT)
-            nc.sync.dma_start(y_rows[:, :, h * HALF:(h + 1) * HALF], y[:])
-            y_grouped = sb.tile([P, HALF, PACK], BF16, name="y_grouped_%d" % h, align_bytes=64)
-            for c in range(0, HALF, P):
-                on_vector = (h * HALF + c) in (0, QUERIES - P)
-                interleave(nc.vector.tensor_copy if on_vector else nc.scalar.copy, y_grouped[:, c:c + P, :], y[:, :, c:c + P])
-            grouped_halves.append(y_grouped)
-        for h in range(2):
+        def round_y(j, engine_copy):
+            h, cols = half_and_columns(j)
+            interleave(engine_copy, y_grouped[j][:], y[h][:, :, cols])
+
+        def quantise_y(j):
             nc.vector.quantize_mx(
-                out=y_codes[:, h * HALF:(h + 1) * HALF].bitcast(FP8X4),
-                scales=y_scales[:, h * HALF:(h + 1) * HALF],
-                in_=grouped_halves[h][:].rearrange("p c t -> p (c t)"),
+                out=y_codes[:, j * P:(j + 1) * P].bitcast(FP8X4),
+                scales=y_scales[:, j * P:(j + 1) * P],
+                in_=y_grouped[j][:].rearrange("p c t -> p (c t)"),
             )
-            nc.sync.dma_start(y_words[:, h * HALF:(h + 1) * HALF], y_codes[:, h * HALF:(h + 1) * HALF])
+
+        round_y(0, nc.vector.tensor_copy)
+        round_y(1, nc.scalar.copy)
+        round_y(2, nc.scalar.copy)
+        quantise_y(0)
+        quantise_y(1)
+        nc.sync.dma_start(y_words[:, 0:HALF], y_codes[:, 0:HALF])
+        round_y(3, nc.vector.tensor_copy)
+        quantise_y(2)
+        quantise_y(3)
+        nc.sync.dma_start(y_words[:, HALF:QUERIES], y_codes[:, HALF:QUERIES])
         for quad in range(4):
             queue = nc.scalar if quad < 2 else nc.sync
             queue.dma_start(

@@ -36,155 +36,163 @@ def tile_attend_plw_mask_topk_kernel(tc, qT, k_words, k_scales, ls, mk, offs, ou
     with ExitStack() as ctx:
         sb = ctx.enter_context(tc.tile_pool(name="sb", bufs=1))
         stage = ctx.enter_context(tc.tile_pool(name="stage", bufs=1))
-        reuse = ctx.enter_context(tc.tile_pool(name="reuse", bufs=1))
         late = ctx.enter_context(tc.tile_pool(name="late", bufs=1))
         ps = ctx.enter_context(tc.psum_pool(name="ps", bufs=BLOCKS))
 
         offsets = sb.tile([P, SLOTS // 16], U16, name="offsets")
         nc.sync.dma_start(offsets[:], offs)
 
-        piece = PACK * HALF
-        ls_rows = sb.tile([P, P], F32, name="ls_rows")
-        nc.gpsimd.memset(ls_rows[:], 0.0)
-        nc.sync.dma_start(ls_rows[0:BLOCKS, :], ls[0, 0].rearrange("(j p) -> j p", p=P))
-
-        pool_scales = reuse.tile([P, PASSES * TOKENS // 4], I32, name="pool_scales", align_bytes=64, offset=0)
-        nc.vector.memset(pool_scales[:], 0)
-        for quad in (0, 2, 1, 3):
-            nc.sync.dma_start(
-                pool_scales[32 * quad:32 * quad + 4, :].rearrange("f (o t) -> f o t", o=PASSES),
-                k_scales.bitcast(I32)[:, 4 * quad:4 * quad + 4, :].rearrange("o f t -> f o t"),
-            )
-
         q_rows = qT[0].rearrange("(o p t) q -> o p t q", p=P, t=PACK)
         mk_rows = mk[0].rearrange("(p r) q -> p r q", r=PACK)
         q_raw, q_codes, q_scales, mask = {}, {}, {}, {}
 
-        def load_q(h, o, place):
-            q_raw[h, o] = place.rearrange("p (t q) -> p t q", t=PACK)
-            nc.sync.dma_start(q_raw[h, o], q_rows[o, :, :, h * HALF:(h + 1) * HALF])
+        def load_q(o, blocks, place):
+            piece = place.rearrange("p (t q) -> p t q", t=PACK)
+            nc.sync.dma_start(piece, q_rows[o, :, :, blocks[0] * P:(blocks[-1] + 1) * P])
+            for n, j in enumerate(blocks):
+                q_raw[j, o] = piece[:, :, n * P:(n + 1) * P]
 
-        def load_mask(h, place):
-            mask[h] = place.rearrange("p (r q) -> p r q", r=PACK)
-            nc.sync.dma_start(mask[h], mk_rows[:, :, h * HALF:(h + 1) * HALF])
+        def load_mask(blocks, place):
+            piece = place.rearrange("p (r q) -> p r q", r=PACK)
+            nc.sync.dma_start(piece, mk_rows[:, :, blocks[0] * P:(blocks[-1] + 1) * P])
+            for n, j in enumerate(blocks):
+                mask[j] = piece[:, :, n * P:(n + 1) * P]
 
-        def quantise_q(h, o, engine_copies, codes):
-            width = HALF // len(engine_copies)
-            grouped = sb.tile([P, HALF, PACK], BF16, name="q_grouped", bufs=2, align_bytes=64)
-            q_codes[h, o] = codes
-            q_scales[h, o] = sb.tile([P, HALF], U8, name="q_scales_%d_%d" % (h, o), align_bytes=64)
-            for c, engine_copy in zip(range(0, HALF, width), engine_copies):
-                interleave(engine_copy, grouped[:, c:c + width, :], q_raw[h, o][:, :, c:c + width])
-            for c in range(0, HALF, width):
-                nc.vector.quantize_mx(
-                    out=q_codes[h, o][:, c:c + width].bitcast(FP8X4),
-                    scales=q_scales[h, o][:, c:c + width],
-                    in_=grouped[:, c:c + width, :].rearrange("p c t -> p (c t)"),
-                )
+        unit = PACK * P
+        first = sb.tile([P, 2 * unit], F32, name="first")
+        load_q(0, [0, 1], first[:])
 
-        first = sb.tile([P, piece], F32, name="first")
-        load_q(0, 0, first[:])
+        scales_place = late.tile([P, 8 * unit], I32, name="scales_place", align_bytes=64, offset=0)
+        pool_scales = scales_place[:, 0:TOKENS // 4]
+        nc.vector.memset(pool_scales, 0)
+        for quad in (0, 2, 1, 3):
+            nc.sync.dma_start(
+                scales_place[32 * quad:32 * quad + 8, 0:TOKENS // 4], k_scales.bitcast(I32)[:, 4 * quad:4 * quad + 4, :]
+            )
 
         identity = sb.tile([P, P], F32, name="identity")
-        blank = stage.tile([P, 7 * piece], F32, name="blank", offset=0)
+        blank = stage.tile([P, 9 * unit], F32, name="blank", align_bytes=64, offset=0)
         nc.gpsimd.memset(blank[:, 0:P], 0.0)
         nc.gpsimd.affine_select(
             out=identity[:], in_=blank[:, 0:P], compare_op=mybir.AluOpType.not_equal, fill=1.0,
             base=0, pattern=[[-1, P]], channel_multiplier=1,
         )
+
+        def staged(pool, name, at, units, dtype=F32):
+            return pool.tile([P, units * unit], dtype, name=name, align_bytes=64, offset=4 * unit * at)
+
+        pool_words = staged(stage, "pool_words", 0, 4, I32)
+        nc.sync.dma_start(pool_words[:], k_words[0].rearrange("p t b -> p (t b)").bitcast(I32))
+
+        ls_rows = sb.tile([P, P], F32, name="ls_rows")
+        nc.gpsimd.memset(ls_rows[:], 0.0)
+        nc.sync.dma_start(ls_rows[0:BLOCKS, :], ls[0, 0].rearrange("(j p) -> j p", p=P))
+        load_q(1, [0, 1], staged(stage, "q_ab1", 4, 2)[:])
+        load_q(0, [2, 3], staged(stage, "q_cd0", 7, 2)[:])
+
+        key_scales = [
+            stage.tile([P, SLOTS], U8, name="key_scales_0", align_bytes=64, offset=4 * unit * 6),
+            sb.tile([P, SLOTS], U8, name="key_scales_1", align_bytes=64),
+        ]
+        nc.vector.memset(key_scales[1][:].bitcast(I32), 0)
+        nc.vector.tensor_copy(key_scales[0][:], pool_scales.bitcast(U8).indirect(offsets[:]))
+        nc.sync.dma_start(key_scales[1][0:100, :].bitcast(I32), key_scales[0][4:104, :].bitcast(I32))
+
+        load_q(1, [2], staged(late, "q_c1", 2, 1)[:])
+        load_q(1, [3], staged(late, "q_d1", 3, 1)[:])
+        load_mask([0, 1], staged(late, "mask_ab", 4, 2)[:])
+        load_mask([2, 3], staged(late, "mask_cd", 6, 2)[:])
+
         ls_turned = ps.tile([P, PACK, P], F32, name="ls_turned", tag="turned")
         nc.tensor.transpose(ls_turned[:, 0, :], ls_rows[:], identity[:])
-        minus_ls = late.tile([P, BLOCKS], F32, name="minus_ls", align_bytes=64, offset=0)
+        minus_ls = sb.tile([P, BLOCKS], F32, name="minus_ls")
         nc.scalar.activation(minus_ls[:], ls_turned[:, 0, 0:BLOCKS], COPY, scale=-1.0)
 
-        pool_words = stage.tile([P, TOKENS], I32, name="pool_words", offset=4 * piece * 5)
-        nc.sync.dma_start(pool_words[:], k_words[0].rearrange("p t b -> p (t b)").bitcast(I32))
-        later = [stage.tile([P, piece], F32, name="later_%d" % n, offset=4 * piece * n) for n in range(5)]
-        load_q(0, 1, later[0][:])
-        load_q(1, 0, later[1][:])
-        load_q(1, 1, later[2][:])
-        load_mask(0, later[3][:])
-        load_mask(1, later[4][:])
+        grouped = {}
 
-        key_scales = []
-        for o in range(PASSES):
-            key_scales.append(sb.tile([P, SLOTS], U8, name="key_scales_%d" % o, align_bytes=64))
-            nc.vector.tensor_copy(
-                key_scales[o][:], pool_scales[:].bitcast(U8)[:, o * TOKENS:(o + 1) * TOKENS].indirect(offsets[:])
-            )
-        key_pairs = reuse.tile([P, SLOTS], U32, name="key_pairs", align_bytes=64, offset=0)
-        nc.vector.tensor_copy(key_pairs[:], pool_words[:].bitcast(U32).indirect(offsets[:]))
-        quantise_q(0, 0, [nc.scalar.copy], reuse.tile([P, HALF], U32, name="q_codes_00", align_bytes=64, offset=8 * HALF))
-        key_codes = []
-        for o in range(PASSES):
-            key_codes.append(sb.tile([P, 2 * SLOTS], U8, name="key_codes_%d" % o, align_bytes=64))
-            nc.vector.tensor_copy(
-                key_codes[o][:].bitcast(U16),
-                key_pairs[:].bitcast(U16).rearrange("p (n o) -> p o n", o=PASSES)[:, o, :],
+        def round_q(j, o, engine_copy, at=None):
+            name = "q_grouped_%d_%d" % (j, o)
+            if at is None:
+                grouped[j, o] = sb.tile([P, P, PACK], BF16, name=name, align_bytes=64)
+            else:
+                grouped[j, o] = stage.tile([P, P, PACK], BF16, name=name, align_bytes=64, offset=2 * unit * at)
+            interleave(engine_copy, grouped[j, o][:], q_raw[j, o])
+
+        def quantise_q(j, o):
+            name = "q_codes_%d_%d" % (j, o)
+            if (j, o) in ((0, 0), (1, 0)):
+                q_codes[j, o] = late.tile([P, P], U32, name=name, align_bytes=64, offset=unit * j)
+            else:
+                q_codes[j, o] = stage.tile([P, P], U32, name=name, align_bytes=64, offset=unit * (6 + 2 * j + o))
+            q_scales[j, o] = sb.tile([P, P], U8, name="q_scales_%d_%d" % (j, o), align_bytes=64)
+            nc.vector.quantize_mx(
+                out=q_codes[j, o][:].bitcast(FP8X4),
+                scales=q_scales[j, o][:],
+                in_=grouped[j, o][:].rearrange("p c t -> p (c t)"),
             )
 
-        quantise_q(0, 1, [nc.scalar.copy], reuse.tile([P, HALF], U32, name="q_codes_01", align_bytes=64, offset=0))
-        quantise_q(1, 0, [nc.scalar.copy], reuse.tile([P, HALF], U32, name="q_codes_10", align_bytes=64, offset=4 * HALF))
-        quantise_q(1, 1, [nc.vector.tensor_copy, nc.scalar.copy], sb.tile([P, HALF], U32, name="q_codes_11", align_bytes=64))
+        round_q(0, 0, nc.scalar.copy)
+        round_q(1, 0, nc.scalar.copy)
+        quantise_q(0, 0)
+        quantise_q(1, 0)
+        run = SLOTS // 2
+        key_pairs = [sb.tile([P, run], U32, name="key_pairs_%d" % n, align_bytes=64) for n in range(2)]
+        key_codes = [sb.tile([P, 2 * SLOTS], U8, name="key_codes_%d" % o, align_bytes=64) for o in range(PASSES)]
 
-        def half_and_columns(j):
-            return j // 2, slice((j % 2) * P, (j % 2 + 1) * P)
+        def split_words(n, o):
+            nc.vector.tensor_copy(
+                key_codes[o][:].bitcast(U16)[:, n * run:(n + 1) * run],
+                key_pairs[n][:].bitcast(U16).rearrange("p (s o) -> p o s", o=PASSES)[:, o, :],
+            )
+
+        for n in range(2):
+            nc.vector.tensor_copy(
+                key_pairs[n][:], pool_words[:].bitcast(U32).indirect(offsets[:, n * run // 16:(n + 1) * run // 16])
+            )
+            split_words(n, 0)
+        for n in range(2):
+            split_words(n, 1)
 
         scores = [ps.tile([P, SLOTS], F32, name="scores") for j in range(BLOCKS)]
         weights = [sb.tile([P, PACK, P], F32, name="weights_%d" % j) for j in range(BLOCKS)]
-        y = [sb.tile([P, PACK, HALF], F32, name="y_%d" % h) for h in range(2)]
+        y_ab = sb.tile([P, PACK, HALF], F32, name="y_ab")
+        y_c = sb.tile([P, PACK, P], F32, name="y_c")
+        y_d = sb.tile([P, PACK, P], F32, name="y_d")
+        y = [y_ab[:, :, 0:P], y_ab[:, :, P:HALF], y_c[:], y_d[:]]
         y_rows = out_0.rearrange("(p r) q -> p r q", r=PACK)
+        y_words = out_1[0].rearrange("p q b -> p (q b)").bitcast(I32)
+        y_codes = sb.tile([P, QUERIES], I32, name="y_codes", align_bytes=64)
+        y_scales = sb.tile([P, QUERIES], U8, name="y_scales", align_bytes=64)
+        y_grouped = [sb.tile([P, P, PACK], BF16, name="y_grouped_%d" % j, align_bytes=64) for j in range(BLOCKS)]
 
-        def score_pass(h, o):
-            for j in (2 * h, 2 * h + 1):
-                cols = half_and_columns(j)[1]
-                nc.tensor.matmul_mx(
-                    out=scores[j][:],
-                    lhsT=q_codes[h, o][:, cols].bitcast(FP8X4),
-                    lhsT_scale=q_scales[h, o][:, cols],
-                    rhs=key_codes[o][:].bitcast(FP4X4),
-                    rhs_scale=key_scales[o][:],
-                    start=(o == 0),
-                    stop=(o == PASSES - 1),
-                )
+        def score_pass(j, o, first=0, count=SLOTS):
+            nc.tensor.matmul_mx(
+                out=scores[j][:, first:first + count],
+                lhsT=q_codes[j, o][:].bitcast(FP8X4),
+                lhsT_scale=q_scales[j, o][:],
+                rhs=key_codes[o][:, 2 * first:2 * (first + count)].bitcast(FP4X4),
+                rhs_scale=key_scales[o][:, first:first + count],
+                start=(o == 0 and first == 0),
+                stop=(o == PASSES - 1),
+            )
 
         def exponentiate(j):
             nc.scalar.activation(
                 weights[j][:], scores[j][:].rearrange("q (s r) -> q r s", r=PACK), EXP, bias=minus_ls[:, j:j + 1]
             )
 
-        def turn_and_mask(j):
-            h, cols = half_and_columns(j)
-            turned = ps.tile([P, PACK, P], F32, name="turned", tag="turned")
+        turned = {}
+
+        def turn(j):
+            turned[j] = ps.tile([P, PACK, P], F32, name="turned", tag="turned")
             for r in range(PACK):
-                nc.tensor.transpose(turned[:, r, :], weights[j][:, r, :], identity[:])
-            nc.vector.tensor_tensor(y[h][:, :, cols], turned[:], mask[h][:, :, cols], MULT)
-            if j % 2 == 1:
-                nc.sync.dma_start(y_rows[:, :, h * HALF:(h + 1) * HALF], y[h][:])
+                nc.tensor.transpose(turned[j][:, r, :], weights[j][:, r, :], identity[:])
 
-        score_pass(0, 0)
-        score_pass(0, 1)
-        score_pass(1, 0)
-        exponentiate(0)
-        exponentiate(1)
-        turn_and_mask(0)
-        score_pass(1, 1)
-        exponentiate(2)
-        exponentiate(3)
-        for j in range(1, BLOCKS):
-            turn_and_mask(j)
-
-        y_words = out_1[0].rearrange("p q b -> p (q b)").bitcast(I32)
-        y_codes = sb.tile([P, QUERIES], I32, name="y_codes", align_bytes=64)
-        y_scales = sb.tile([P, QUERIES], U8, name="y_scales", align_bytes=64)
-        y_grouped = [
-            late.tile([P, P, PACK], BF16, name="y_grouped_%d" % j, align_bytes=64, offset=2 * P * PACK * ((j - 1) % BLOCKS))
-            for j in range(BLOCKS)
-        ]
+        def apply_mask(j):
+            nc.vector.tensor_tensor(y[j], turned[j][:], mask[j], MULT)
 
         def round_y(j, engine_copy):
-            h, cols = half_and_columns(j)
-            interleave(engine_copy, y_grouped[j][:], y[h][:, :, cols])
+            interleave(engine_copy, y_grouped[j][:], y[j])
 
         def quantise_y(j):
             nc.vector.quantize_mx(
@@ -193,12 +201,48 @@ def tile_attend_plw_mask_topk_kernel(tc, qT, k_words, k_scales, ls, mk, offs, ou
                 in_=y_grouped[j][:].rearrange("p c t -> p (c t)"),
             )
 
-        round_y(0, nc.vector.tensor_copy)
+        for n in range(2):
+            score_pass(0, 0, n * run, run)
+            score_pass(1, 0, n * run, run)
+        round_q(0, 1, nc.scalar.copy)
+        round_q(1, 1, nc.scalar.copy)
+        quantise_q(0, 1)
+        quantise_q(1, 1)
+        score_pass(0, 1)
+        score_pass(1, 1)
+        round_q(2, 0, nc.scalar.copy)
+        round_q(3, 0, nc.vector.tensor_copy, 0)
+        exponentiate(0)
+        quantise_q(3, 0)
+        quantise_q(2, 0)
+        exponentiate(1)
+        round_q(2, 1, nc.vector.tensor_copy, 1)
+        round_q(3, 1, nc.vector.tensor_copy, 2)
+        quantise_q(2, 1)
+        quantise_q(3, 1)
+        score_pass(2, 0)
+        score_pass(3, 0)
+        turn(0)
+        score_pass(2, 1)
+        score_pass(3, 1)
+        exponentiate(2)
+        exponentiate(3)
+        turn(1)
+        apply_mask(0)
+        apply_mask(1)
+        nc.sync.dma_start(y_rows[:, :, 0:HALF], y_ab[:])
+        turn(2)
+        turn(3)
+        round_y(0, nc.scalar.copy)
         round_y(1, nc.scalar.copy)
-        round_y(2, nc.scalar.copy)
+        apply_mask(2)
+        nc.sync.dma_start(y_rows[:, :, HALF:HALF + P], y_c[:])
         quantise_y(0)
+        apply_mask(3)
+        nc.sync.dma_start(y_rows[:, :, HALF + P:QUERIES], y_d[:])
         quantise_y(1)
         nc.sync.dma_start(y_words[:, 0:HALF], y_codes[:, 0:HALF])
+        round_y(2, nc.scalar.copy)
         round_y(3, nc.vector.tensor_copy)
         quantise_y(2)
         quantise_y(3)

@@ -65,10 +65,9 @@ def tile_attend_plw_mask_topk_kernel(tc, qT, k_words, k_scales, ls, mk, offs, ou
         scales_place = late.tile([P, 8 * unit], I32, name="scales_place", align_bytes=64, offset=0)
         pool_scales = scales_place[:, 0:TOKENS // 4]
         nc.vector.memset(pool_scales, 0)
-        for quad in (0, 2, 1, 3):
-            nc.sync.dma_start(
-                scales_place[32 * quad:32 * quad + 8, 0:TOKENS // 4], k_scales.bitcast(I32)[:, 4 * quad:4 * quad + 4, :]
-            )
+        scale_rows = k_scales.bitcast(I32).rearrange("o (g j) t -> j g o t", j=4)
+        for j in range(4):
+            nc.sync.dma_start(scales_place[j:P:16, 0:TOKENS // 4], scale_rows[j])
 
         identity = sb.tile([P, P], F32, name="identity")
         blank = stage.tile([P, 9 * unit], F32, name="blank", align_bytes=64, offset=0)
@@ -96,11 +95,12 @@ def tile_attend_plw_mask_topk_kernel(tc, qT, k_words, k_scales, ls, mk, offs, ou
         ]
         nc.vector.memset(key_scales[1][:].bitcast(I32), 0)
         nc.vector.tensor_copy(key_scales[0][:], pool_scales.bitcast(U8).indirect(offsets[:]))
-        nc.sync.dma_start(key_scales[1][0:100, :].bitcast(I32), key_scales[0][4:104, :].bitcast(I32))
+        nc.sync.dma_start(key_scales[1][0:100, :].bitcast(I32), key_scales[0][16:116, :].bitcast(I32))
 
         load_q(1, [2], staged(late, "q_c1", 2, 1)[:])
         load_q(1, [3], staged(late, "q_d1", 3, 1)[:])
-        load_mask([0, 1], staged(late, "mask_ab", 4, 2)[:])
+        load_mask([0], staged(late, "mask_a", 4, 1)[:])
+        load_mask([1], staged(late, "mask_b", 5, 1)[:])
         load_mask([2, 3], staged(late, "mask_cd", 6, 2)[:])
 
         ls_turned = ps.tile([P, PACK, P], F32, name="ls_turned", tag="turned")
@@ -155,10 +155,7 @@ def tile_attend_plw_mask_topk_kernel(tc, qT, k_words, k_scales, ls, mk, offs, ou
 
         scores = [ps.tile([P, SLOTS], F32, name="scores") for j in range(BLOCKS)]
         weights = [sb.tile([P, PACK, P], F32, name="weights_%d" % j) for j in range(BLOCKS)]
-        y_ab = sb.tile([P, PACK, HALF], F32, name="y_ab")
-        y_c = sb.tile([P, PACK, P], F32, name="y_c")
-        y_d = sb.tile([P, PACK, P], F32, name="y_d")
-        y = [y_ab[:, :, 0:P], y_ab[:, :, P:HALF], y_c[:], y_d[:]]
+        y = [sb.tile([P, PACK, P], F32, name="y_%d" % j)[:] for j in range(BLOCKS)]
         y_rows = out_0.rearrange("(p r) q -> p r q", r=PACK)
         y_words = out_1[0].rearrange("p q b -> p (q b)").bitcast(I32)
         y_codes = sb.tile([P, QUERIES], I32, name="y_codes", align_bytes=64)
@@ -176,23 +173,26 @@ def tile_attend_plw_mask_topk_kernel(tc, qT, k_words, k_scales, ls, mk, offs, ou
                 stop=(o == PASSES - 1),
             )
 
-        def exponentiate(j):
+        def exponentiate(j, places=range(PACK)):
+            rows = slice(places[0], places[-1] + 1)
             nc.scalar.activation(
-                weights[j][:], scores[j][:].rearrange("q (s r) -> q r s", r=PACK), EXP, bias=minus_ls[:, j:j + 1]
+                weights[j][:, rows, :], scores[j][:].rearrange("q (s r) -> q r s", r=PACK)[:, rows, :], EXP,
+                bias=minus_ls[:, j:j + 1],
             )
 
         turned = {}
 
-        def turn(j):
-            turned[j] = ps.tile([P, PACK, P], F32, name="turned", tag="turned")
-            for r in range(PACK):
-                nc.tensor.transpose(turned[j][:, r, :], weights[j][:, r, :], identity[:])
+        def turn(j, places=range(PACK), tag="turned"):
+            turned[j, places[0]] = ps.tile([P, PACK, P], F32, name="turned", tag=tag)
+            for r in places:
+                nc.tensor.transpose(turned[j, places[0]][:, r, :], weights[j][:, r, :], identity[:])
 
-        def apply_mask(j):
-            nc.vector.tensor_tensor(y[j], turned[j][:], mask[j], MULT)
+        def apply_mask(j, places=range(PACK)):
+            rows = slice(places[0], places[-1] + 1)
+            nc.vector.tensor_tensor(y[j][:, rows, :], turned[j, places[0]][:, rows, :], mask[j][:, rows, :], MULT)
 
-        def round_y(j, engine_copy):
-            interleave(engine_copy, y_grouped[j][:], y[j])
+        def round_y(j, engine_copy, first=0, count=P):
+            interleave(engine_copy, y_grouped[j][:, first:first + count, :], y[j][:, :, first:first + count])
 
         def quantise_y(j):
             nc.vector.quantize_mx(
@@ -201,9 +201,22 @@ def tile_attend_plw_mask_topk_kernel(tc, qT, k_words, k_scales, ls, mk, offs, ou
                 in_=y_grouped[j][:].rearrange("p c t -> p (c t)"),
             )
 
+        for j in range(2):
+            nc.tensor.matmul_mx(
+                out=scores[2 + j][:],
+                lhsT=q_codes[j, 0][:].bitcast(FP8X4),
+                lhsT_scale=q_scales[j, 0][:],
+                rhs=pool_words[:].bitcast(U8)[:, 0:2 * SLOTS].bitcast(FP4X4),
+                rhs_scale=key_scales[0][:],
+                start=True,
+                stop=True,
+            )
         for n in range(2):
             score_pass(0, 0, n * run, run)
             score_pass(1, 0, n * run, run)
+        def store_y(j):
+            nc.sync.dma_start(y_rows[:, :, j * P:(j + 1) * P], y[j])
+
         round_q(0, 1, nc.scalar.copy)
         round_q(1, 1, nc.scalar.copy)
         quantise_q(0, 1)
@@ -213,37 +226,42 @@ def tile_attend_plw_mask_topk_kernel(tc, qT, k_words, k_scales, ls, mk, offs, ou
         round_q(2, 0, nc.scalar.copy)
         round_q(3, 0, nc.vector.tensor_copy, 0)
         exponentiate(0)
-        quantise_q(3, 0)
         quantise_q(2, 0)
+        quantise_q(3, 0)
         exponentiate(1)
         round_q(2, 1, nc.vector.tensor_copy, 1)
         round_q(3, 1, nc.vector.tensor_copy, 2)
         quantise_q(2, 1)
         quantise_q(3, 1)
+        turn(0)
         score_pass(2, 0)
         score_pass(3, 0)
-        turn(0)
         score_pass(2, 1)
         score_pass(3, 1)
         exponentiate(2)
-        exponentiate(3)
+        exponentiate(3, range(0, 2))
+        exponentiate(3, range(2, 4))
         turn(1)
         apply_mask(0)
+        store_y(0)
+        round_y(0, nc.vector.tensor_copy)
         apply_mask(1)
-        nc.sync.dma_start(y_rows[:, :, 0:HALF], y_ab[:])
+        store_y(1)
         turn(2)
-        turn(3)
-        round_y(0, nc.scalar.copy)
+        turn(3, range(0, 2))
+        turn(3, range(2, 4), "scores")
         round_y(1, nc.scalar.copy)
         apply_mask(2)
-        nc.sync.dma_start(y_rows[:, :, HALF:HALF + P], y_c[:])
+        store_y(2)
+        apply_mask(3, range(0, 2))
+        apply_mask(3, range(2, 4))
+        store_y(3)
+        round_y(2, nc.scalar.copy)
+        round_y(3, nc.vector.tensor_copy, 0, P // 2)
+        round_y(3, nc.scalar.copy, P // 2, P // 2)
         quantise_y(0)
-        apply_mask(3)
-        nc.sync.dma_start(y_rows[:, :, HALF + P:QUERIES], y_d[:])
         quantise_y(1)
         nc.sync.dma_start(y_words[:, 0:HALF], y_codes[:, 0:HALF])
-        round_y(2, nc.scalar.copy)
-        round_y(3, nc.vector.tensor_copy)
         quantise_y(2)
         quantise_y(3)
         nc.sync.dma_start(y_words[:, HALF:QUERIES], y_codes[:, HALF:QUERIES])

@@ -62,16 +62,17 @@ def tile_attend_plw_mask_topk_kernel(tc, qT, k_words, k_scales, ls, mk, offs, ou
         first = sb.tile([P, 2 * unit], F32, name="first")
         load_q(0, [0, 1], first[:])
 
+        identity = sb.tile([P, P], F32, name="identity")
+        blank = stage.tile([P, 9 * unit], F32, name="blank", align_bytes=64, offset=0)
+        nc.vector.memset(blank[:, 0:P], 0.0)
+
         scales_place = late.tile([P, 8 * unit], I32, name="scales_place", align_bytes=64, offset=0)
         pool_scales = scales_place[:, 0:TOKENS // 4]
-        nc.vector.memset(pool_scales, 0)
+        nc.gpsimd.memset(pool_scales, 0)
         scale_rows = k_scales.bitcast(I32).rearrange("o (g j) t -> j g o t", j=4)
         for j in range(4):
             nc.sync.dma_start(scales_place[j:P:16, 0:TOKENS // 4], scale_rows[j])
 
-        identity = sb.tile([P, P], F32, name="identity")
-        blank = stage.tile([P, 9 * unit], F32, name="blank", align_bytes=64, offset=0)
-        nc.gpsimd.memset(blank[:, 0:P], 0.0)
         nc.gpsimd.affine_select(
             out=identity[:], in_=blank[:, 0:P], compare_op=mybir.AluOpType.not_equal, fill=1.0,
             base=0, pattern=[[-1, P]], channel_multiplier=1,
@@ -84,7 +85,7 @@ def tile_attend_plw_mask_topk_kernel(tc, qT, k_words, k_scales, ls, mk, offs, ou
         nc.sync.dma_start(pool_words[:], k_words[0].rearrange("p t b -> p (t b)").bitcast(I32))
 
         ls_rows = sb.tile([P, P], F32, name="ls_rows")
-        nc.gpsimd.memset(ls_rows[:], 0.0)
+        nc.vector.memset(ls_rows[:], 0.0)
         nc.sync.dma_start(ls_rows[0:BLOCKS, :], ls[0, 0].rearrange("(j p) -> j p", p=P))
         load_q(1, [0, 1], staged(stage, "q_ab1", 4, 2)[:])
         load_q(0, [2, 3], staged(stage, "q_cd0", 7, 2)[:])
@@ -261,10 +262,10 @@ def tile_attend_plw_mask_topk_kernel(tc, qT, k_words, k_scales, ls, mk, offs, ou
         round_y(3, nc.scalar.copy, P // 2, P // 2)
         quantise_y(0)
         quantise_y(1)
-        nc.sync.dma_start(y_words[:, 0:HALF], y_codes[:, 0:HALF])
         quantise_y(2)
+        nc.sync.dma_start(y_words[:, 0:3 * P], y_codes[:, 0:3 * P])
         quantise_y(3)
-        nc.sync.dma_start(y_words[:, HALF:QUERIES], y_codes[:, HALF:QUERIES])
+        nc.sync.dma_start(y_words[:, 3 * P:QUERIES], y_codes[:, 3 * P:QUERIES])
         for quad in range(4):
             queue = nc.scalar if quad < 2 else nc.sync
             queue.dma_start(

@@ -150,9 +150,9 @@ def tile_attend_plw_mask_topk_kernel(tc, qT, k_words, k_scales, ls, mk, offs, ou
             nc.vector.tensor_copy(
                 key_pairs[n][:], pool_words[:].bitcast(U32).indirect(offsets[:, n * run // 16:(n + 1) * run // 16])
             )
-            split_words(n, 0)
         for n in range(2):
-            split_words(n, 1)
+            for o in range(PASSES):
+                split_words(n, o)
 
         scores = [ps.tile([P, SLOTS], F32, name="scores") for j in range(BLOCKS)]
         weights = [sb.tile([P, PACK, P], F32, name="weights_%d" % j) for j in range(BLOCKS)]
@@ -258,14 +258,13 @@ def tile_attend_plw_mask_topk_kernel(tc, qT, k_words, k_scales, ls, mk, offs, ou
         apply_mask(3, range(2, 4))
         store_y(3)
         round_y(2, nc.scalar.copy)
-        round_y(3, nc.vector.tensor_copy, 0, P // 2)
-        round_y(3, nc.scalar.copy, P // 2, P // 2)
         quantise_y(0)
         quantise_y(1)
+        round_y(3, nc.vector.tensor_copy, 0, P // 2)
+        round_y(3, nc.scalar.copy, P // 2, P // 2)
         quantise_y(2)
-        nc.sync.dma_start(y_words[:, 0:3 * P], y_codes[:, 0:3 * P])
         quantise_y(3)
-        nc.sync.dma_start(y_words[:, 3 * P:QUERIES], y_codes[:, 3 * P:QUERIES])
+        nc.sync.dma_start(y_words, y_codes[:])
         for quad in range(4):
             queue = nc.scalar if quad < 2 else nc.sync
             queue.dma_start(

from contextlib import ExitStack

import concourse.mybir as mybir

SLOTS, TOKENS, FEATURES, QUERIES = 512, 2048, 1024, 512
FLOPS = 2 * SLOTS * FEATURES * QUERIES

F32 = mybir.dt.float32
BF16 = mybir.dt.bfloat16
I32 = mybir.dt.int32
U32 = mybir.dt.uint32
U16 = mybir.dt.uint16
U8 = mybir.dt.uint8
FP8X4 = mybir.dt.float8_e4m3fn_x4
FP4X4 = mybir.dt.float4_e2m1fn_x4
EXP = mybir.ActivationFunctionType.Exp
COPY = mybir.ActivationFunctionType.Copy
MULT = mybir.AluOpType.mult

P = 128
PACK = 4
PASSES = FEATURES // (P * PACK)
HALF = QUERIES // 2
BLOCKS = QUERIES // P


def interleave(engine_copy, dst, src):
    engine_copy(
        dst.rearrange("p (c i) t -> p c t i", i=PACK),
        src.rearrange("p t (c i) -> p c t i", i=PACK),
    )


def tile_attend_plw_mask_topk_kernel(tc, qT, k_words, k_scales, ls, mk, offs, out_0, out_1, out_2):
    nc = tc.nc
    with ExitStack() as ctx:
        sb = ctx.enter_context(tc.tile_pool(name="sb", bufs=1))
        stage = ctx.enter_context(tc.tile_pool(name="stage", bufs=1))
        late = ctx.enter_context(tc.tile_pool(name="late", bufs=1))
        ps = ctx.enter_context(tc.psum_pool(name="ps", bufs=BLOCKS))

        offsets = sb.tile([P, SLOTS // 16], U16, name="offsets")
        nc.sync.dma_start(offsets[:], offs)

        q_rows = qT[0].rearrange("(o p t) q -> o p t q", p=P, t=PACK)
        mk_rows = mk[0].rearrange("(p r) q -> p r q", r=PACK)
        q_raw, q_codes, q_scales, mask = {}, {}, {}, {}

        def load_q(o, blocks, place):
            piece = place.rearrange("p (t q) -> p t q", t=PACK)
            nc.sync.dma_start(piece, q_rows[o, :, :, blocks[0] * P:(blocks[-1] + 1) * P])
            for n, j in enumerate(blocks):
                q_raw[j, o] = piece[:, :, n * P:(n + 1) * P]

        def load_mask(blocks, place):
            piece = place.rearrange("p (r q) -> p r q", r=PACK)
            nc.sync.dma_start(piece, mk_rows[:, :, blocks[0] * P:(blocks[-1] + 1) * P])
            for n, j in enumerate(blocks):
                mask[j] = piece[:, :, n * P:(n + 1) * P]

        unit = PACK * P
        first = sb.tile([P, 2 * unit], F32, name="first")
        load_q(0, [0, 1], first[:])

        identity = sb.tile([P, P], F32, name="identity")
        blank = stage.tile([P, 9 * unit], F32, name="blank", align_bytes=64, offset=0)
        nc.vector.memset(blank[:, 0:P], 0.0)

        scales_place = late.tile([P, 8 * unit], I32, name="scales_place", align_bytes=64, offset=0)
        pool_scales = scales_place[:, 0:TOKENS // 4]
        nc.gpsimd.memset(pool_scales, 0)
        scale_rows = k_scales.bitcast(I32).rearrange("o (g j) t -> j g o t", j=4)
        for j in range(4):
            nc.sync.dma_start(scales_place[j:P:16, 0:TOKENS // 4], scale_rows[j])

        nc.gpsimd.affine_select(
            out=identity[:], in_=blank[:, 0:P], compare_op=mybir.AluOpType.not_equal, fill=1.0,
            base=0, pattern=[[-1, P]], channel_multiplier=1,
        )

        def staged(pool, name, at, units, dtype=F32):
            return pool.tile([P, units * unit], dtype, name=name, align_bytes=64, offset=4 * unit * at)

        pool_words = staged(stage, "pool_words", 0, 4, I32)
        nc.sync.dma_start(pool_words[:], k_words[0].rearrange("p t b -> p (t b)").bitcast(I32))

        ls_rows = sb.tile([P, P], F32, name="ls_rows")
        nc.vector.memset(ls_rows[:], 0.0)
        nc.sync.dma_start(ls_rows[0:BLOCKS, :], ls[0, 0].rearrange("(j p) -> j p", p=P))
        load_q(1, [0, 1], staged(stage, "q_ab1", 4, 2)[:])
        load_q(0, [2, 3], staged(stage, "q_cd0", 7, 2)[:])

        key_scales = [
            stage.tile([P, SLOTS], U8, name="key_scales_0", align_bytes=64, offset=4 * unit * 6),
            sb.tile([P, SLOTS], U8, name="key_scales_1", align_bytes=64),
        ]
        nc.vector.memset(key_scales[1][:].bitcast(I32), 0)
        nc.vector.tensor_copy(key_scales[0][:], pool_scales.bitcast(U8).indirect(offsets[:]))
        nc.sync.dma_start(key_scales[1][0:100, :].bitcast(I32), key_scales[0][16:116, :].bitcast(I32))

        load_q(1, [2], staged(late, "q_c1", 2, 1)[:])
        load_q(1, [3], staged(late, "q_d1", 3, 1)[:])
        load_mask([0], staged(late, "mask_a", 4, 1)[:])
        load_mask([1], staged(late, "mask_b", 5, 1)[:])
        load_mask([2, 3], staged(late, "mask_cd", 6, 2)[:])

        ls_turned = ps.tile([P, PACK, P], F32, name="ls_turned", tag="turned")
        nc.tensor.transpose(ls_turned[:, 0, :], ls_rows[:], identity[:])
        minus_ls = sb.tile([P, BLOCKS], F32, name="minus_ls")
        nc.scalar.activation(minus_ls[:], ls_turned[:, 0, 0:BLOCKS], COPY, scale=-1.0)

        grouped = {}

        def round_q(j, o, engine_copy, at=None):
            name = "q_grouped_%d_%d" % (j, o)
            if at is None:
                grouped[j, o] = sb.tile([P, P, PACK], BF16, name=name, align_bytes=64)
            else:
                grouped[j, o] = stage.tile([P, P, PACK], BF16, name=name, align_bytes=64, offset=2 * unit * at)
            interleave(engine_copy, grouped[j, o][:], q_raw[j, o])

        def quantise_q(j, o):
            name = "q_codes_%d_%d" % (j, o)
            if (j, o) in ((0, 0), (1, 0)):
                q_codes[j, o] = late.tile([P, P], U32, name=name, align_bytes=64, offset=unit * j)
            else:
                q_codes[j, o] = stage.tile([P, P], U32, name=name, align_bytes=64, offset=unit * (6 + 2 * j + o))
            q_scales[j, o] = sb.tile([P, P], U8, name="q_scales_%d_%d" % (j, o), align_bytes=64)
            nc.vector.quantize_mx(
                out=q_codes[j, o][:].bitcast(FP8X4),
                scales=q_scales[j, o][:],
                in_=grouped[j, o][:].rearrange("p c t -> p (c t)"),
            )

        round_q(0, 0, nc.scalar.copy)
        round_q(1, 0, nc.scalar.copy)
        quantise_q(0, 0)
        quantise_q(1, 0)
        run = SLOTS // 2
        key_pairs = [sb.tile([P, run], U32, name="key_pairs_%d" % n, align_bytes=64) for n in range(2)]
        key_codes = [sb.tile([P, 2 * SLOTS], U8, name="key_codes_%d" % o, align_bytes=64) for o in range(PASSES)]

        def split_words(n, o):
            nc.vector.tensor_copy(
                key_codes[o][:].bitcast(U16)[:, n * run:(n + 1) * run],
                key_pairs[n][:].bitcast(U16).rearrange("p (s o) -> p o s", o=PASSES)[:, o, :],
            )

        for n in range(2):
            nc.vector.tensor_copy(
                key_pairs[n][:], pool_words[:].bitcast(U32).indirect(offsets[:, n * run // 16:(n + 1) * run // 16])
            )
        for n in range(2):
            for o in range(PASSES):
                split_words(n, o)

        scores = [ps.tile([P, SLOTS], F32, name="scores") for j in range(BLOCKS)]
        weights = [sb.tile([P, PACK, P], F32, name="weights_%d" % j) for j in range(BLOCKS)]
        y = [sb.tile([P, PACK, P], F32, name="y_%d" % j)[:] for j in range(BLOCKS)]
        y_rows = out_0.rearrange("(p r) q -> p r q", r=PACK)
        y_words = out_1[0].rearrange("p q b -> p (q b)").bitcast(I32)
        y_codes = sb.tile([P, QUERIES], I32, name="y_codes", align_bytes=64)
        y_scales = sb.tile([P, QUERIES], U8, name="y_scales", align_bytes=64)
        y_grouped = [sb.tile([P, P, PACK], BF16, name="y_grouped_%d" % j, align_bytes=64) for j in range(BLOCKS)]

        def score_pass(j, o, first=0, count=SLOTS):
            nc.tensor.matmul_mx(
                out=scores[j][:, first:first + count],
                lhsT=q_codes[j, o][:].bitcast(FP8X4),
                lhsT_scale=q_scales[j, o][:],
                rhs=key_codes[o][:, 2 * first:2 * (first + count)].bitcast(FP4X4),
                rhs_scale=key_scales[o][:, first:first + count],
                start=(o == 0 and first == 0),
                stop=(o == PASSES - 1),
            )

        def exponentiate(j, places=range(PACK)):
            rows = slice(places[0], places[-1] + 1)
            nc.scalar.activation(
                weights[j][:, rows, :], scores[j][:].rearrange("q (s r) -> q r s", r=PACK)[:, rows, :], EXP,
                bias=minus_ls[:, j:j + 1],
            )

        turned = {}

        def turn(j, places=range(PACK), tag="turned"):
            turned[j, places[0]] = ps.tile([P, PACK, P], F32, name="turned", tag=tag)
            for r in places:
                nc.tensor.transpose(turned[j, places[0]][:, r, :], weights[j][:, r, :], identity[:])

        def apply_mask(j, places=range(PACK)):
            rows = slice(places[0], places[-1] + 1)
            nc.vector.tensor_tensor(y[j][:, rows, :], turned[j, places[0]][:, rows, :], mask[j][:, rows, :], MULT)

        def round_y(j, engine_copy, first=0, count=P):
            interleave(engine_copy, y_grouped[j][:, first:first + count, :], y[j][:, :, first:first + count])

        def quantise_y(j):
            nc.vector.quantize_mx(
                out=y_codes[:, j * P:(j + 1) * P].bitcast(FP8X4),
                scales=y_scales[:, j * P:(j + 1) * P],
                in_=y_grouped[j][:].rearrange("p c t -> p (c t)"),
            )

        for j in range(2):
            nc.tensor.matmul_mx(
                out=scores[2 + j][:],
                lhsT=q_codes[j, 0][:].bitcast(FP8X4),
                lhsT_scale=q_scales[j, 0][:],
                rhs=pool_words[:].bitcast(U8)[:, 0:2 * SLOTS].bitcast(FP4X4),
                rhs_scale=key_scales[0][:],
                start=True,
                stop=True,
            )
        for n in range(2):
            score_pass(0, 0, n * run, run)
            score_pass(1, 0, n * run, run)
        def store_y(j):
            nc.sync.dma_start(y_rows[:, :, j * P:(j + 1) * P], y[j])

        round_q(0, 1, nc.scalar.copy)
        round_q(1, 1, nc.scalar.copy)
        quantise_q(0, 1)
        quantise_q(1, 1)
        score_pass(0, 1)
        score_pass(1, 1)
        round_q(2, 0, nc.scalar.copy)
        round_q(3, 0, nc.vector.tensor_copy, 0)
        exponentiate(0)
        quantise_q(2, 0)
        quantise_q(3, 0)
        exponentiate(1)
        round_q(2, 1, nc.vector.tensor_copy, 1)
        round_q(3, 1, nc.vector.tensor_copy, 2)
        quantise_q(2, 1)
        quantise_q(3, 1)
        turn(0)
        score_pass(2, 0)
        score_pass(3, 0)
        score_pass(2, 1)
        score_pass(3, 1)
        exponentiate(2)
        exponentiate(3, range(0, 2))
        exponentiate(3, range(2, 4))
        turn(1)
        apply_mask(0)
        store_y(0)
        round_y(0, nc.vector.tensor_copy)
        apply_mask(1)
        store_y(1)
        turn(2)
        turn(3, range(0, 2))
        turn(3, range(2, 4), "scores")
        round_y(1, nc.scalar.copy)
        apply_mask(2)
        store_y(2)
        apply_mask(3, range(0, 2))
        apply_mask(3, range(2, 4))
        store_y(3)
        round_y(2, nc.scalar.copy)
        quantise_y(0)
        quantise_y(1)
        round_y(3, nc.vector.tensor_copy, 0, P // 2)
        round_y(3, nc.scalar.copy, P // 2, P // 2)
        quantise_y(2)
        quantise_y(3)
        nc.sync.dma_start(y_words, y_codes[:])
        for quad in range(4):
            queue = nc.scalar if quad < 2 else nc.sync
            queue.dma_start(
                out_2[0].bitcast(I32)[4 * quad:4 * quad + 4, :], y_scales[32 * quad:32 * quad + 4, :].bitcast(I32)
            )
